import numpy as np
import ml_dtypes


def mxq(x, axis, fmt="e4m3"):
    dtype, down = {"e4m3": (ml_dtypes.float8_e4m3fn, 7), "e5m2": (ml_dtypes.float8_e5m2, 14)}[fmt]
    v = np.moveaxis(np.asarray(x, np.float32).astype(ml_dtypes.bfloat16).astype(np.float64), axis, -1)
    blocks = v.reshape(v.shape[:-1] + (-1, 32))
    amax = np.abs(blocks).max(-1, keepdims=True)
    byte = np.maximum(np.where(amax > 0, np.frexp(amax)[1] - 1 + 127, 0) - down, 1)
    scale = np.exp2(byte - 127.0)
    codes = (blocks / scale).astype(np.float32).astype(dtype).astype(np.float64)
    return np.moveaxis((codes * scale).reshape(v.shape), -1, axis)


WIDE = False


def mx_kscale(k):
    if not WIDE:
        return np.ones(k)
    levels = np.array([10, -10, 5, -5, 0])
    if k % 512:
        return np.exp2(np.random.permutation(np.resize(levels, k // 32))).repeat(32)
    a = np.empty((k // 512, 16))
    for p in range(k // 512):
        a[p, :8] = np.random.permutation(np.resize(levels, 8))
        for g in range(8):
            far = levels[np.abs(levels - a[p, g]) >= 10]
            a[p, g + 8] = far[np.random.randint(len(far))]
    return np.exp2(a.ravel()).repeat(32)


def f64(x):
    return np.asarray(x).astype(np.float64)


def striped(idx):
    return np.tile(idx.reshape(-1, 16).T, (8, 1)).astype(np.uint16)


def unstriped(offs):
    return offs[:16].T.reshape(-1).astype(np.int64)


def striped8(idx):
    return np.concatenate([x.reshape(-1, 16).T for x in idx]).astype(np.uint16)


def runs(offs, k):
    lists = np.stack([offs[16 * r : 16 * r + 16].T.reshape(-1) for r in range(8)]).astype(np.int64)
    return lists[np.arange(k) % 512 // 64]


def pack_weight(w):
    k, n = w.shape
    w = f64(np.asarray(w, np.float32).astype(ml_dtypes.bfloat16)).reshape(k // 32, 32, n)
    amax = np.abs(w).max(1)
    byte = np.clip(np.where(amax > 0, np.frexp(amax)[1] - 1 + 127 - 7, 1), 1, 254)
    scaled = (w * np.exp2(127.0 - byte)[:, None, :]).reshape(k, n).astype(np.float32)
    words = np.ascontiguousarray(scaled.reshape(k // 512, 128, 4, n).transpose(0, 1, 3, 2)).astype(ml_dtypes.float8_e4m3fn).view(np.uint8)
    return words, np.ascontiguousarray(byte.astype(np.uint8).reshape(k // 512, 16, n))


def unpack_weight(words, scales):
    g, p, n, _ = words.shape
    vals = np.ascontiguousarray(words).view(ml_dtypes.float8_e4m3fn).astype(np.float64) * np.repeat(np.exp2(scales.astype(np.float64) - 127.0), 8, axis=1)[..., None]
    return vals.transpose(0, 1, 3, 2).reshape(g * 512, n)


def sigmoid(v):
    return 1.0 / (1.0 + np.exp(-np.maximum(v, -700.0)))


K, T, S, G, H, U = 512, 2048, 512, 2048, 512, 1024


def setup_inputs():
    n = np.random.standard_normal
    s = mx_kscale(K)[:, None]
    packed_xT = pack_weight(n((K, T)) * s)
    packed_dT = pack_weight(n((K, G)) / s)
    return {
        "x_words": packed_xT[0],
        "x_scales": packed_xT[1],
        "d_words": packed_dT[0],
        "d_scales": packed_dT[1],
        "gs": (np.random.uniform(0.5, 1.5, (K, 1)) * s).astype(np.float32),
        "mem": n((H, U)).astype(np.float32),
        "offs": striped(np.random.permutation(T)[:S]),
        "k1": striped8(np.random.randint(0, G, (8, H))),
        "n1": striped8(np.stack([np.random.permutation(S) for _ in range(8)])),
        "n2": striped8(np.stack([np.random.permutation(S) for _ in range(8)])),
        "n3": striped8(np.stack([np.random.permutation(U)[:S] for _ in range(8)])),
    }


def reference(x_words, x_scales, d_words, d_scales, gs, mem, offs, k1, n1, n2, n3):
    old = f64(mem)[np.arange(H)[:, None], runs(n3, H)]
    d_k1 = unpack_weight(d_words, d_scales)[np.arange(K)[:, None], runs(k1, K)]
    xq = unpack_weight(x_words, x_scales)[:, unstriped(offs)]
    h = 0.0625 * (d_k1.T @ xq)
    z = f64(gs) * (h - (np.minimum(h[np.arange(H)[:, None], runs(n1, H)], h[np.arange(H)[:, None], runs(n2, H)])))
    h2 = 0.0625 * ((d_k1.T @ mxq(z, 0, "e4m3")))
    nw = old + sigmoid(h2) * (h2 - old)
    out = f64(mem).copy()
    out[np.arange(H)[:, None], runs(n3, H)] = nw
    return out

@@ -1,0 +1,193 @@
+from contextlib import ExitStack
+
+import concourse.mybir as mybir
+
+F32 = mybir.dt.float32
+BF16 = mybir.dt.bfloat16
+I32 = mybir.dt.int32
+U32 = mybir.dt.uint32
+U16 = mybir.dt.uint16
+U8 = mybir.dt.uint8
+FP8X4 = mybir.dt.float8_e4m3fn_x4
+ALU = mybir.AluOpType
+ACT = mybir.ActivationFunctionType
+
+P = 128
+PACK = 4
+K, T, S, G, H, U = 512, 2048, 512, 2048, 512, 1024
+HALF = S // 2
+LCOL = HALF // 16
+FLOPS = 2 * 2 * K * H * S
+
+
+def tile_picked_ringunderpaget_none_p_kernel(tc, x_words, x_scales, d_words, d_scales, gs, mem, offs, k1, n1, n2, n3, out):
+    nc = tc.nc
+    with ExitStack() as ctx:
+        lists = ctx.enter_context(tc.tile_pool(name="lists", bufs=1))
+        big = ctx.enter_context(tc.tile_pool(name="big", bufs=1))
+        keep = ctx.enter_context(tc.tile_pool(name="keep", bufs=1))
+        psum = ctx.enter_context(tc.psum_pool(name="psum", bufs=1))
+
+        def load_list(src, name):
+            lst = lists.tile([P, S // 16], U16, name=name)
+            nc.sync.dma_start(lst[:], src)
+            return lst
+
+        d_sc_win = keep.tile([P, G], U8, align_bytes=64)
+        x_sc_win = keep.tile([P, T], U8, align_bytes=64)
+        nc.gpsimd.memset(d_sc_win[:].bitcast(I32), 0)
+        nc.vector.memset(x_sc_win[:].bitcast(I32), 0)
+
+        k1_l = load_list(k1, "k1_l")
+        offs_l = load_list(offs, "offs_l")
+        n1_l = load_list(n1, "n1_l")
+        n2_l = load_list(n2, "n2_l")
+        nc.scalar.dma_start(d_sc_win[0:P:8, :].bitcast(I32), d_scales[0].bitcast(I32))
+        nc.scalar.dma_start(x_sc_win[0:P:8, :].bitcast(I32), x_scales[0].bitcast(I32))
+        d_win = big.tile([P, G], U32, offset=0)
+        x_win = big.tile([P, T], U32, offset=4 * G)
+        nc.sync.dma_start(d_win[:].bitcast(I32), d_words[0].rearrange("p n t -> p (n t)").bitcast(I32))
+        nc.sync.dma_start(x_win[:].bitcast(I32), x_words[0].rearrange("p n t -> p (n t)").bitcast(I32))
+        n3_l = load_list(n3, "n3_l")
+        gs_t = keep.tile([P, PACK], F32)
+        nc.gpsimd.dma_start(gs_t[:], gs.rearrange("(p t) o -> p (t o)", t=PACK))
+        mem_rows = mem.rearrange("(p t) u -> t p u", t=PACK)
+        out_rows = out.rearrange("(p t) u -> t p u", t=PACK)
+
+        d_sc_got = keep.tile([P, H], U8, align_bytes=64)
+        nc.vector.tensor_copy(d_sc_got[:], d_sc_win[:].indirect(k1_l[:]))
+        planes = keep.tile([P, H + S], U8, align_bytes=64)
+        nc.vector.tensor_copy(planes[:, 0:H].rearrange("p (t m) -> p m t", t=PACK), d_sc_got[:].rearrange("p (m t) -> p m t", t=PACK))
+        x_sc_got = keep.tile([P, S], U8, align_bytes=64)
+        nc.vector.tensor_copy(x_sc_got[:], x_sc_win[:].indirect(offs_l[:]))
+        nc.vector.tensor_copy(planes[:, H : H + S].bitcast(I32), x_sc_got[:].bitcast(I32))
+        for a in range(1, 4):
+            nc.scalar.dma_start(planes[a:P:32, :].bitcast(I32), planes[8 * a : P : 32, :].bitcast(I32))
+        d_sc = planes[:, 0:H]
+        x_sc = planes[:, H : H + S]
+        d_got = keep.tile([P, H], U32, align_bytes=64)
+        nc.vector.tensor_copy(d_got[:], d_win[:].indirect(k1_l[:]))
+        d_codes = keep.tile([P, H], U32, align_bytes=64)
+        nc.vector.tensor_copy(
+            d_codes[:].rearrange("p (t c i) -> p c t i", t=PACK, i=4),
+            d_got[:].rearrange("p (c i t) -> p c t i", t=PACK, i=4),
+        )
+
+        x_codes = keep.tile([P, S], U32, align_bytes=64)
+        h_ps = [psum.tile([P, S], F32, name=f"h_ps{t}") for t in range(PACK)]
+        for c in range(2):
+            cols = slice(c * HALF, (c + 1) * HALF)
+            nc.vector.tensor_copy(x_codes[:, cols], x_win[:].indirect(offs_l[:, c * LCOL : (c + 1) * LCOL]))
+        for t in range(PACK):
+            for c in range(2):
+                cols = slice(c * HALF, (c + 1) * HALF)
+                rows = slice(t * P, (t + 1) * P)
+                nc.tensor.matmul_mx(
+                    out=h_ps[t][:, cols], lhsT=d_codes[:, rows].bitcast(FP8X4), lhsT_scale=d_sc[:, rows],
+                    rhs=x_codes[:, cols].bitcast(FP8X4), rhs_scale=x_sc[:, cols], start=True, stop=True,
+                )
+
+        page = []
+        for t in range(PACK):
+            page_t = big.tile([P, U], F32, name=f"page{t}", offset=4 * U * t)
+            nc.sync.dma_start(page_t[:], mem_rows[t])
+            page.append(page_t)
+
+        h = [keep.tile([P, S], F32, name=f"h{t}") for t in range(PACK)]
+        for t in range(PACK):
+            if t % 2 == 0:
+                nc.scalar.activation(h[t][:], h_ps[t][:], ACT.Copy, scale=0.0625)
+            else:
+                nc.vector.tensor_scalar(h[t][:], h_ps[t][:], 0.0625, None, ALU.mult)
+
+        got = {}
+        half_old = {}
+        diff = [keep.tile([P, PACK, HALF], F32, name=f"diff{c}") for c in range(2)]
+        h2_ps = {}
+        th = {}
+        new = {}
+
+        def fetch(c, t, w, dst, on_vector):
+            window = h[t][:].indirect((n1_l, n2_l)[w][:, c * LCOL : (c + 1) * LCOL])
+            if on_vector:
+                nc.vector.tensor_copy(dst, window)
+            else:
+                nc.scalar.activation(dst, window, ACT.Copy)
+            got[c, t, w] = dst
+
+        def fetch_old(t, dst):
+            nc.scalar.activation(dst, page[t][:].indirect(n3_l[:]), ACT.Copy, scale=0.5)
+
+        def make_z(c, t):
+            low = keep.tile([P, HALF], F32, name=f"low{c}{t}")
+            nc.vector.tensor_tensor(low[:], got[c, t, 0], got[c, t, 1], ALU.min)
+            nc.vector.tensor_tensor(diff[c][:, t, :], h[t][:, c * HALF : (c + 1) * HALF], low[:], ALU.subtract)
+
+        def second_product(c):
+            z_il = keep.tile([P, HALF, PACK], BF16, name=f"z_il{c}", tag=f"z_il{c}", align_bytes=64)
+            nc.vector.tensor_tensor(
+                z_il[:].rearrange("p (c i) t -> p c t i", i=4),
+                diff[c][:].rearrange("p t (c i) -> p c t i", i=4),
+                gs_t[:].unsqueeze(1).unsqueeze(3).broadcast_to([P, HALF // 4, PACK, 4]),
+                ALU.mult,
+            )
+            z_codes = keep.tile([P, HALF], U32, name=f"z_codes{c}", align_bytes=64)
+            z_sc = keep.tile([P, HALF], U8, name=f"z_sc{c}", align_bytes=64)
+            nc.vector.quantize_mx(z_codes[:].bitcast(FP8X4), z_sc[:], z_il[:].rearrange("p j t -> p (j t)"))
+            for pair in range(2):
+                bank = psum.tile([P, 2, HALF], F32, name=f"h2_ps{c}{pair}")
+                h2_ps[c, pair] = bank
+                for u in range(2):
+                    rows = slice((2 * pair + u) * P, (2 * pair + u + 1) * P)
+                    nc.tensor.matmul_mx(
+                        out=bank[:, u, :], lhsT=d_codes[:, rows].bitcast(FP8X4), lhsT_scale=d_sc[:, rows],
+                        rhs=z_codes[:].bitcast(FP8X4), rhs_scale=z_sc[:], start=True, stop=True,
+                    )
+
+        def gate(c, pair, tag):
+            bank = h2_ps[c, pair]
+            th[c, pair] = keep.tile([P, 2, HALF], F32, name=f"th{c}{pair}", tag=tag)
+            nc.scalar.activation(th[c, pair][:], bank[:], ACT.Tanh, scale=-0.03125)
+            new[c, pair] = keep.tile([P, 2, HALF], F32, name=f"new{c}{pair}")
+            nc.scalar.activation(new[c, pair][:], bank[:], ACT.Silu, scale=0.0625)
+
+        def put(c, pair, tag):
+            cols = slice(c * HALF, (c + 1) * HALF)
+            lcols = slice(c * LCOL, (c + 1) * LCOL)
+            kept = keep.tile([P, 2, HALF], F32, name=f"kept{c}{pair}", tag=tag, align_bytes=64)
+            nc.vector.scalar_tensor_tensor(kept[:], th[c, pair][:], 1.0, half_old[pair][:, :, cols], ALU.add, ALU.mult)
+            for u in range(2):
+                t = 2 * pair + u
+                nc.vector.tensor_tensor(page[t][:].indirect(n3_l[:, lcols]), kept[:, u, :], new[c, pair][:, u, :], ALU.add)
+                if c == 1:
+                    nc.sync.dma_start(out_rows[t], page[t][:])
+
+        got_a = keep.tile([P, 2 * PACK, HALF], F32, tag="got_a")
+        for t in range(PACK):
+            for w in range(2):
+                fetch(0, t, w, got_a[:, 2 * t + w, :], (t, w) in ((1, 0), (1, 1), (3, 1)))
+            make_z(0, t)
+        second_product(0)
+        got_b = keep.tile([P, 2 * PACK, HALF], F32)
+        for t in range(PACK):
+            for w in range(2):
+                fetch(1, t, w, got_b[:, 2 * t + w, :], False)
+            make_z(1, t)
+        second_product(1)
+
+        def fetch_old_pair(pair, tag):
+            old = keep.tile([P, 2, S], F32, name=f"old{pair}", tag=tag)
+            half_old[pair] = old[:]
+            for u in range(2):
+                fetch_old(2 * pair + u, old[:, u, :])
+
+        gate(0, 0, "th00")
+        fetch_old_pair(0, "got_a")
+        put(0, 0, "z_il1")
+        gate(0, 1, "th01")
+        fetch_old_pair(1, "th00")
+        put(0, 1, "kept01")
+        gate(1, 0, "th10")
+        put(1, 0, "kept10")
+        gate(1, 1, "th11")
+        put(1, 1, "kept11")

@@ -33,24 +33,28 @@ def tile_picked_ringunderpaget_none_p_kernel(tc, x_words, x_scales, d_words, d_s
             nc.sync.dma_start(lst[:], src)
             return lst
 
-        d_sc_win = keep.tile([P, G], U8, align_bytes=64)
-        x_sc_win = keep.tile([P, T], U8, align_bytes=64)
-        nc.gpsimd.memset(d_sc_win[:].bitcast(I32), 0)
-        nc.vector.memset(x_sc_win[:].bitcast(I32), 0)
+        def load_scales(src, width, name):
+            win = keep.tile([P, width], U8, name=name, align_bytes=64)
+            nc.sync.dma_start(win[:].bitcast(I32), src[0].bitcast(I32).unsqueeze(1).broadcast_to([16, 8, width // 4]))
+            return win
+
+        warm = keep.tile([P, 2], F32)
+        nc.vector.memset(warm[:], 0.0)
+        nc.scalar.activation(warm[:, 1:2], warm[:, 0:1], ACT.Silu)
 
         k1_l = load_list(k1, "k1_l")
+        d_sc_win = load_scales(d_scales, G, "d_sc_win")
         offs_l = load_list(offs, "offs_l")
-        n1_l = load_list(n1, "n1_l")
-        n2_l = load_list(n2, "n2_l")
-        nc.scalar.dma_start(d_sc_win[0:P:8, :].bitcast(I32), d_scales[0].bitcast(I32))
-        nc.scalar.dma_start(x_sc_win[0:P:8, :].bitcast(I32), x_scales[0].bitcast(I32))
+        x_sc_win = load_scales(x_scales, T, "x_sc_win")
         d_win = big.tile([P, G], U32, offset=0)
         x_win = big.tile([P, T], U32, offset=4 * G)
         nc.sync.dma_start(d_win[:].bitcast(I32), d_words[0].rearrange("p n t -> p (n t)").bitcast(I32))
         nc.sync.dma_start(x_win[:].bitcast(I32), x_words[0].rearrange("p n t -> p (n t)").bitcast(I32))
+        n1_l = load_list(n1, "n1_l")
+        n2_l = load_list(n2, "n2_l")
         n3_l = load_list(n3, "n3_l")
         gs_t = keep.tile([P, PACK], F32)
-        nc.gpsimd.dma_start(gs_t[:], gs.rearrange("(p t) o -> p (t o)", t=PACK))
+        nc.sync.dma_start(gs_t[:], gs.rearrange("(p t) o -> p (t o)", t=PACK))
         mem_rows = mem.rearrange("(p t) u -> t p u", t=PACK)
         out_rows = out.rearrange("(p t) u -> t p u", t=PACK)
 
@@ -102,7 +106,12 @@ def tile_picked_ringunderpaget_none_p_kernel(tc, x_words, x_scales, d_words, d_s
 
         got = {}
         half_old = {}
-        diff = [keep.tile([P, PACK, HALF], F32, name=f"diff{c}") for c in range(2)]
+        z = [keep.tile([P, PACK, HALF], BF16, name=f"z{c}") for c in range(2)]
+        neg_gs = keep.tile([P, PACK], F32)
+        nc.gpsimd.tensor_scalar(neg_gs[:], gs_t[:], -1.0, 0.0, ALU.mult, ALU.add)
+        gh = [keep.tile([P, S], F32, name=f"gh{t}") for t in range(PACK)]
+        for t in range(PACK):
+            nc.gpsimd.tensor_scalar(gh[t][:], h[t][:], gs_t[:, t : t + 1], 0.0, ALU.mult, ALU.add)
         h2_ps = {}
         th = {}
         new = {}
@@ -121,18 +130,15 @@ def tile_picked_ringunderpaget_none_p_kernel(tc, x_words, x_scales, d_words, d_s
         def make_z(c, t):
             low = keep.tile([P, HALF], F32, name=f"low{c}{t}")
             nc.vector.tensor_tensor(low[:], got[c, t, 0], got[c, t, 1], ALU.min)
-            nc.vector.tensor_tensor(diff[c][:, t, :], h[t][:, c * HALF : (c + 1) * HALF], low[:], ALU.subtract)
+            nc.vector.scalar_tensor_tensor(z[c][:, t, :], low[:], neg_gs[:, t : t + 1], gh[t][:, c * HALF : (c + 1) * HALF], ALU.mult, ALU.add)
 
         def second_product(c):
             z_il = keep.tile([P, HALF, PACK], BF16, name=f"z_il{c}", tag=f"z_il{c}", align_bytes=64)
-            nc.vector.tensor_tensor(
-                z_il[:].rearrange("p (c i) t -> p c t i", i=4),
-                diff[c][:].rearrange("p t (c i) -> p c t i", i=4),
-                gs_t[:].unsqueeze(1).unsqueeze(3).broadcast_to([P, HALF // 4, PACK, 4]),
-                ALU.mult,
+            nc.vector.tensor_copy(
+                z_il[:].rearrange("p (c i) t -> p c t i", i=4), z[c][:].rearrange("p t (c i) -> p c t i", i=4)
             )
-            z_codes = keep.tile([P, HALF], U32, name=f"z_codes{c}", align_bytes=64)
-            z_sc = keep.tile([P, HALF], U8, name=f"z_sc{c}", align_bytes=64)
+            z_codes = keep.tile([P, HALF], U32, name=f"z_codes{c}", tag=f"z_codes{c}", align_bytes=64)
+            z_sc = keep.tile([P, HALF], U8, name=f"z_sc{c}", tag=f"z_sc{c}", align_bytes=64)
             nc.vector.quantize_mx(z_codes[:].bitcast(FP8X4), z_sc[:], z_il[:].rearrange("p j t -> p (j t)"))
             for pair in range(2):
                 bank = psum.tile([P, 2, HALF], F32, name=f"h2_ps{c}{pair}")
@@ -144,23 +150,38 @@ def tile_picked_ringunderpaget_none_p_kernel(tc, x_words, x_scales, d_words, d_s
                         rhs=z_codes[:].bitcast(FP8X4), rhs_scale=z_sc[:], start=True, stop=True,
                     )
 
-        def gate(c, pair, tag):
+        def gate(c, pair, tag, new_tag):
             bank = h2_ps[c, pair]
-            th[c, pair] = keep.tile([P, 2, HALF], F32, name=f"th{c}{pair}", tag=tag)
-            nc.scalar.activation(th[c, pair][:], bank[:], ACT.Tanh, scale=-0.03125)
-            new[c, pair] = keep.tile([P, 2, HALF], F32, name=f"new{c}{pair}")
+            new[c, pair] = keep.tile([P, 2, HALF], F32, name=f"new{c}{pair}", tag=new_tag, align_bytes=64)
             nc.scalar.activation(new[c, pair][:], bank[:], ACT.Silu, scale=0.0625)
+            th[c, pair] = keep.tile([P, 2, HALF], F32, name=f"th{c}{pair}", tag=tag, align_bytes=64)
+            nc.scalar.activation(th[c, pair][:], bank[:], ACT.Tanh, scale=-0.03125)
 
-        def put(c, pair, tag):
+        nw = [keep.tile([P, S], F32, name=f"nw{t}") for t in range(PACK)]
+
+        def blend(c, pair):
             cols = slice(c * HALF, (c + 1) * HALF)
-            lcols = slice(c * LCOL, (c + 1) * LCOL)
-            kept = keep.tile([P, 2, HALF], F32, name=f"kept{c}{pair}", tag=tag, align_bytes=64)
-            nc.vector.scalar_tensor_tensor(kept[:], th[c, pair][:], 1.0, half_old[pair][:, :, cols], ALU.add, ALU.mult)
+            if (c, pair) != (0, 0):
+                th1 = keep.tile([P, 2, HALF], F32, name=f"th1{c}{pair}")
+                nc.scalar.activation(th1[:], th[c, pair][:], ACT.Copy, bias=1.0)
             for u in range(2):
                 t = 2 * pair + u
-                nc.vector.tensor_tensor(page[t][:].indirect(n3_l[:, lcols]), kept[:, u, :], new[c, pair][:, u, :], ALU.add)
-                if c == 1:
-                    nc.sync.dma_start(out_rows[t], page[t][:])
+                if (c, pair) == (0, 0):
+                    kept = keep.tile([P, HALF], F32, name=f"kept_v{u}", tag=("z_il1", "kept_v1")[u], align_bytes=64)
+                    nc.vector.scalar_tensor_tensor(kept[:], th[c, pair][:, u, :], 1.0, half_old[t][:, cols], ALU.add, ALU.mult)
+                    if u == 0:
+                        nc.vector.tensor_tensor(page[0][:].indirect(n3_l[:, 0:LCOL]), kept[:], new[c, pair][:, u, :], ALU.add)
+                    else:
+                        nc.vector.tensor_tensor(nw[t][:, cols], kept[:], new[c, pair][:, u, :], ALU.add)
+                else:
+                    kept = keep.tile([P, HALF], F32, name="kept_g")
+                    nc.gpsimd.tensor_tensor(kept[:], th1[:, u, :], half_old[t][:, cols], ALU.mult)
+                    nc.gpsimd.tensor_tensor(nw[t][:, cols], kept[:], new[c, pair][:, u, :], ALU.add)
+
+        def put(t, c0, c1):
+            nc.vector.tensor_copy(page[t][:].indirect(n3_l[:, c0 * LCOL : c1 * LCOL]), nw[t][:, c0 * HALF : c1 * HALF])
+            if c1 == 2:
+                nc.sync.dma_start(out_rows[t], page[t][:])
 
         got_a = keep.tile([P, 2 * PACK, HALF], F32, tag="got_a")
         for t in range(PACK):
@@ -171,23 +192,31 @@ def tile_picked_ringunderpaget_none_p_kernel(tc, x_words, x_scales, d_words, d_s
         got_b = keep.tile([P, 2 * PACK, HALF], F32)
         for t in range(PACK):
             for w in range(2):
-                fetch(1, t, w, got_b[:, 2 * t + w, :], False)
+                fetch(1, t, w, got_b[:, 2 * t + w, :], (t, w) == (3, 1))
             make_z(1, t)
         second_product(1)
 
-        def fetch_old_pair(pair, tag):
-            old = keep.tile([P, 2, S], F32, name=f"old{pair}", tag=tag)
-            half_old[pair] = old[:]
-            for u in range(2):
-                fetch_old(2 * pair + u, old[:, u, :])
-
-        gate(0, 0, "th00")
-        fetch_old_pair(0, "got_a")
-        put(0, 0, "z_il1")
-        gate(0, 1, "th01")
-        fetch_old_pair(1, "th00")
-        put(0, 1, "kept01")
-        gate(1, 0, "th10")
-        put(1, 0, "kept10")
-        gate(1, 1, "th11")
-        put(1, 1, "kept11")
+        gate(0, 0, "th00", "new00")
+        old0 = keep.tile([P, S], F32)
+        old1 = keep.tile([P, S], F32, tag="z_codes0", align_bytes=64)
+        half_old[0], half_old[1] = old0[:], old1[:]
+        fetch_old(0, old0[:])
+        fetch_old(1, old1[:])
+        blend(0, 0)
+        put(1, 0, 1)
+        gate(1, 0, "th10", "new10")
+        blend(1, 0)
+        put(0, 1, 2)
+        put(1, 1, 2)
+        gate(0, 1, "z_sc1", "z_codes1")
+        old23 = keep.tile([P, 2, S], F32, tag="th10", align_bytes=64)
+        half_old[2], half_old[3] = old23[:, 0, :], old23[:, 1, :]
+        fetch_old(2, old23[:, 0, :])
+        fetch_old(3, old23[:, 1, :])
+        blend(0, 1)
+        put(2, 0, 1)
+        put(3, 0, 1)
+        gate(1, 1, "th11", "new11")
+        blend(1, 1)
+        put(2, 1, 2)
+        put(3, 1, 2)

@@ -153,21 +153,23 @@ def tile_picked_ringunderpaget_none_p_kernel(tc, x_words, x_scales, d_words, d_s
         def gate(c, pair, tag, new_tag):
             bank = h2_ps[c, pair]
             new[c, pair] = keep.tile([P, 2, HALF], F32, name=f"new{c}{pair}", tag=new_tag, align_bytes=64)
-            nc.scalar.activation(new[c, pair][:], bank[:], ACT.Silu, scale=0.0625)
             th[c, pair] = keep.tile([P, 2, HALF], F32, name=f"th{c}{pair}", tag=tag, align_bytes=64)
             nc.scalar.activation(th[c, pair][:], bank[:], ACT.Tanh, scale=-0.03125)
+            nc.scalar.activation(new[c, pair][:], bank[:], ACT.Silu, scale=0.0625)
 
         nw = [keep.tile([P, S], F32, name=f"nw{t}") for t in range(PACK)]
 
         def blend(c, pair):
             cols = slice(c * HALF, (c + 1) * HALF)
-            if (c, pair) != (0, 0):
-                th1 = keep.tile([P, 2, HALF], F32, name=f"th1{c}{pair}")
+            if (c, pair) == (0, 0):
+                kept_v = keep.tile([P, 2, HALF], F32, tag="z_il1", align_bytes=64)
+            else:
+                th1 = keep.tile([P, 2, HALF], F32, name=f"th1{c}{pair}", tag=f"th1{c}{pair}", align_bytes=64)
                 nc.scalar.activation(th1[:], th[c, pair][:], ACT.Copy, bias=1.0)
             for u in range(2):
                 t = 2 * pair + u
                 if (c, pair) == (0, 0):
-                    kept = keep.tile([P, HALF], F32, name=f"kept_v{u}", tag=("z_il1", "kept_v1")[u], align_bytes=64)
+                    kept = kept_v[:, u, :]
                     nc.vector.scalar_tensor_tensor(kept[:], th[c, pair][:, u, :], 1.0, half_old[t][:, cols], ALU.add, ALU.mult)
                     if u == 0:
                         nc.vector.tensor_tensor(page[0][:].indirect(n3_l[:, 0:LCOL]), kept[:], new[c, pair][:, u, :], ALU.add)
@@ -216,7 +218,7 @@ def tile_picked_ringunderpaget_none_p_kernel(tc, x_words, x_scales, d_words, d_s
         blend(0, 1)
         put(2, 0, 1)
         put(3, 0, 1)
-        gate(1, 1, "th11", "new11")
+        gate(1, 1, "th110", "new10")
         blend(1, 1)
         put(2, 1, 2)
         put(3, 1, 2)

from contextlib import ExitStack

import concourse.mybir as mybir

F32 = mybir.dt.float32
BF16 = mybir.dt.bfloat16
I32 = mybir.dt.int32
U32 = mybir.dt.uint32
U16 = mybir.dt.uint16
U8 = mybir.dt.uint8
FP8X4 = mybir.dt.float8_e4m3fn_x4
ALU = mybir.AluOpType
ACT = mybir.ActivationFunctionType

P = 128
PACK = 4
K, T, S, G, H, U = 512, 2048, 512, 2048, 512, 1024
HALF = S // 2
LCOL = HALF // 16
FLOPS = 2 * 2 * K * H * S


def tile_picked_ringunderpaget_none_p_kernel(tc, x_words, x_scales, d_words, d_scales, gs, mem, offs, k1, n1, n2, n3, out):
    nc = tc.nc
    with ExitStack() as ctx:
        lists = ctx.enter_context(tc.tile_pool(name="lists", bufs=1))
        big = ctx.enter_context(tc.tile_pool(name="big", bufs=1))
        keep = ctx.enter_context(tc.tile_pool(name="keep", bufs=1))
        psum = ctx.enter_context(tc.psum_pool(name="psum", bufs=1))

        def load_list(src, name):
            lst = lists.tile([P, S // 16], U16, name=name)
            nc.sync.dma_start(lst[:], src)
            return lst

        def load_scales(src, width, name):
            win = keep.tile([P, width], U8, name=name, align_bytes=64)
            nc.sync.dma_start(win[:].bitcast(I32), src[0].bitcast(I32).unsqueeze(1).broadcast_to([16, 8, width // 4]))
            return win

        warm = keep.tile([P, 2], F32)
        nc.vector.memset(warm[:], 0.0)
        nc.scalar.activation(warm[:, 1:2], warm[:, 0:1], ACT.Silu)

        k1_l = load_list(k1, "k1_l")
        d_sc_win = load_scales(d_scales, G, "d_sc_win")
        offs_l = load_list(offs, "offs_l")
        x_sc_win = load_scales(x_scales, T, "x_sc_win")
        d_win = big.tile([P, G], U32, offset=0)
        x_win = big.tile([P, T], U32, offset=4 * G)
        nc.sync.dma_start(d_win[:].bitcast(I32), d_words[0].rearrange("p n t -> p (n t)").bitcast(I32))
        nc.sync.dma_start(x_win[:].bitcast(I32), x_words[0].rearrange("p n t -> p (n t)").bitcast(I32))
        n1_l = load_list(n1, "n1_l")
        n2_l = load_list(n2, "n2_l")
        n3_l = load_list(n3, "n3_l")
        gs_t = keep.tile([P, PACK], F32)
        nc.sync.dma_start(gs_t[:], gs.rearrange("(p t) o -> p (t o)", t=PACK))
        mem_rows = mem.rearrange("(p t) u -> t p u", t=PACK)
        out_rows = out.rearrange("(p t) u -> t p u", t=PACK)

        d_sc_got = keep.tile([P, H], U8, align_bytes=64)
        nc.vector.tensor_copy(d_sc_got[:], d_sc_win[:].indirect(k1_l[:]))
        planes = keep.tile([P, H + S], U8, align_bytes=64)
        nc.vector.tensor_copy(planes[:, 0:H].rearrange("p (t m) -> p m t", t=PACK), d_sc_got[:].rearrange("p (m t) -> p m t", t=PACK))
        x_sc_got = keep.tile([P, S], U8, align_bytes=64)
        nc.vector.tensor_copy(x_sc_got[:], x_sc_win[:].indirect(offs_l[:]))
        nc.vector.tensor_copy(planes[:, H : H + S].bitcast(I32), x_sc_got[:].bitcast(I32))
        for a in range(1, 4):
            nc.scalar.dma_start(planes[a:P:32, :].bitcast(I32), planes[8 * a : P : 32, :].bitcast(I32))
        d_sc = planes[:, 0:H]
        x_sc = planes[:, H : H + S]
        d_got = keep.tile([P, H], U32, align_bytes=64)
        nc.vector.tensor_copy(d_got[:], d_win[:].indirect(k1_l[:]))
        d_codes = keep.tile([P, H], U32, align_bytes=64)
        nc.vector.tensor_copy(
            d_codes[:].rearrange("p (t c i) -> p c t i", t=PACK, i=4),
            d_got[:].rearrange("p (c i t) -> p c t i", t=PACK, i=4),
        )

        x_codes = keep.tile([P, S], U32, align_bytes=64)
        h_ps = [psum.tile([P, S], F32, name=f"h_ps{t}") for t in range(PACK)]
        for c in range(2):
            cols = slice(c * HALF, (c + 1) * HALF)
            nc.vector.tensor_copy(x_codes[:, cols], x_win[:].indirect(offs_l[:, c * LCOL : (c + 1) * LCOL]))
        for t in range(PACK):
            for c in range(2):
                cols = slice(c * HALF, (c + 1) * HALF)
                rows = slice(t * P, (t + 1) * P)
                nc.tensor.matmul_mx(
                    out=h_ps[t][:, cols], lhsT=d_codes[:, rows].bitcast(FP8X4), lhsT_scale=d_sc[:, rows],
                    rhs=x_codes[:, cols].bitcast(FP8X4), rhs_scale=x_sc[:, cols], start=True, stop=True,
                )

        page = []
        for t in range(PACK):
            page_t = big.tile([P, U], F32, name=f"page{t}", offset=4 * U * t)
            nc.sync.dma_start(page_t[:], mem_rows[t])
            page.append(page_t)

        h = [keep.tile([P, S], F32, name=f"h{t}") for t in range(PACK)]
        for t in range(PACK):
            if t % 2 == 0:
                nc.scalar.activation(h[t][:], h_ps[t][:], ACT.Copy, scale=0.0625)
            else:
                nc.vector.tensor_scalar(h[t][:], h_ps[t][:], 0.0625, None, ALU.mult)

        got = {}
        half_old = {}
        z = [keep.tile([P, PACK, HALF], BF16, name=f"z{c}") for c in range(2)]
        neg_gs = keep.tile([P, PACK], F32)
        nc.gpsimd.tensor_scalar(neg_gs[:], gs_t[:], -1.0, 0.0, ALU.mult, ALU.add)
        gh = [keep.tile([P, S], F32, name=f"gh{t}") for t in range(PACK)]
        for t in range(PACK):
            nc.gpsimd.tensor_scalar(gh[t][:], h[t][:], gs_t[:, t : t + 1], 0.0, ALU.mult, ALU.add)
        h2_ps = {}
        th = {}
        new = {}

        def fetch(c, t, w, dst, on_vector):
            window = h[t][:].indirect((n1_l, n2_l)[w][:, c * LCOL : (c + 1) * LCOL])
            if on_vector:
                nc.vector.tensor_copy(dst, window)
            else:
                nc.scalar.activation(dst, window, ACT.Copy)
            got[c, t, w] = dst

        def fetch_old(t, dst):
            nc.scalar.activation(dst, page[t][:].indirect(n3_l[:]), ACT.Copy, scale=0.5)

        def make_z(c, t):
            low = keep.tile([P, HALF], F32, name=f"low{c}{t}")
            nc.vector.tensor_tensor(low[:], got[c, t, 0], got[c, t, 1], ALU.min)
            nc.vector.scalar_tensor_tensor(z[c][:, t, :], low[:], neg_gs[:, t : t + 1], gh[t][:, c * HALF : (c + 1) * HALF], ALU.mult, ALU.add)

        def second_product(c):
            z_il = keep.tile([P, HALF, PACK], BF16, name=f"z_il{c}", tag=f"z_il{c}", align_bytes=64)
            nc.vector.tensor_copy(
                z_il[:].rearrange("p (c i) t -> p c t i", i=4), z[c][:].rearrange("p t (c i) -> p c t i", i=4)
            )
            z_codes = keep.tile([P, HALF], U32, name=f"z_codes{c}", tag=f"z_codes{c}", align_bytes=64)
            z_sc = keep.tile([P, HALF], U8, name=f"z_sc{c}", tag=f"z_sc{c}", align_bytes=64)
            nc.vector.quantize_mx(z_codes[:].bitcast(FP8X4), z_sc[:], z_il[:].rearrange("p j t -> p (j t)"))
            for pair in range(2):
                bank = psum.tile([P, 2, HALF], F32, name=f"h2_ps{c}{pair}")
                h2_ps[c, pair] = bank
                for u in range(2):
                    rows = slice((2 * pair + u) * P, (2 * pair + u + 1) * P)
                    nc.tensor.matmul_mx(
                        out=bank[:, u, :], lhsT=d_codes[:, rows].bitcast(FP8X4), lhsT_scale=d_sc[:, rows],
                        rhs=z_codes[:].bitcast(FP8X4), rhs_scale=z_sc[:], start=True, stop=True,
                    )

        def gate(c, pair, tag, new_tag):
            bank = h2_ps[c, pair]
            new[c, pair] = keep.tile([P, 2, HALF], F32, name=f"new{c}{pair}", tag=new_tag, align_bytes=64)
            th[c, pair] = keep.tile([P, 2, HALF], F32, name=f"th{c}{pair}", tag=tag, align_bytes=64)
            nc.scalar.activation(th[c, pair][:], bank[:], ACT.Tanh, scale=-0.03125)
            nc.scalar.activation(new[c, pair][:], bank[:], ACT.Silu, scale=0.0625)

        nw = [keep.tile([P, S], F32, name=f"nw{t}") for t in range(PACK)]

        def blend(c, pair):
            cols = slice(c * HALF, (c + 1) * HALF)
            if (c, pair) == (0, 0):
                kept_v = keep.tile([P, 2, HALF], F32, tag="z_il1", align_bytes=64)
            else:
                th1 = keep.tile([P, 2, HALF], F32, name=f"th1{c}{pair}", tag=f"th1{c}{pair}", align_bytes=64)
                nc.scalar.activation(th1[:], th[c, pair][:], ACT.Copy, bias=1.0)
            for u in range(2):
                t = 2 * pair + u
                if (c, pair) == (0, 0):
                    kept = kept_v[:, u, :]
                    nc.vector.scalar_tensor_tensor(kept[:], th[c, pair][:, u, :], 1.0, half_old[t][:, cols], ALU.add, ALU.mult)
                    if u == 0:
                        nc.vector.tensor_tensor(page[0][:].indirect(n3_l[:, 0:LCOL]), kept[:], new[c, pair][:, u, :], ALU.add)
                    else:
                        nc.vector.tensor_tensor(nw[t][:, cols], kept[:], new[c, pair][:, u, :], ALU.add)
                else:
                    kept = keep.tile([P, HALF], F32, name="kept_g")
                    nc.gpsimd.tensor_tensor(kept[:], th1[:, u, :], half_old[t][:, cols], ALU.mult)
                    nc.gpsimd.tensor_tensor(nw[t][:, cols], kept[:], new[c, pair][:, u, :], ALU.add)

        def put(t, c0, c1):
            nc.vector.tensor_copy(page[t][:].indirect(n3_l[:, c0 * LCOL : c1 * LCOL]), nw[t][:, c0 * HALF : c1 * HALF])
            if c1 == 2:
                nc.sync.dma_start(out_rows[t], page[t][:])

        got_a = keep.tile([P, 2 * PACK, HALF], F32, tag="got_a")
        for t in range(PACK):
            for w in range(2):
                fetch(0, t, w, got_a[:, 2 * t + w, :], (t, w) in ((1, 0), (1, 1), (3, 1)))
            make_z(0, t)
        second_product(0)
        got_b = keep.tile([P, 2 * PACK, HALF], F32)
        for t in range(PACK):
            for w in range(2):
                fetch(1, t, w, got_b[:, 2 * t + w, :], (t, w) == (3, 1))
            make_z(1, t)
        second_product(1)

        gate(0, 0, "th00", "new00")
        old0 = keep.tile([P, S], F32)
        old1 = keep.tile([P, S], F32, tag="z_codes0", align_bytes=64)
        half_old[0], half_old[1] = old0[:], old1[:]
        fetch_old(0, old0[:])
        fetch_old(1, old1[:])
        blend(0, 0)
        put(1, 0, 1)
        gate(1, 0, "th10", "new10")
        blend(1, 0)
        put(0, 1, 2)
        put(1, 1, 2)
        gate(0, 1, "z_sc1", "z_codes1")
        old23 = keep.tile([P, 2, S], F32, tag="th10", align_bytes=64)
        half_old[2], half_old[3] = old23[:, 0, :], old23[:, 1, :]
        fetch_old(2, old23[:, 0, :])
        fetch_old(3, old23[:, 1, :])
        blend(0, 1)
        put(2, 0, 1)
        put(3, 0, 1)
        gate(1, 1, "th110", "new10")
        blend(1, 1)
        put(2, 1, 2)
        put(3, 1, 2)
